import numpy as np
import ml_dtypes


def mxq(x, axis, fmt="e4m3"):
    dtype, down = {"e4m3": (ml_dtypes.float8_e4m3fn, 7), "e5m2": (ml_dtypes.float8_e5m2, 14)}[fmt]
    v = np.moveaxis(np.asarray(x, np.float32).astype(ml_dtypes.bfloat16).astype(np.float64), axis, -1)
    blocks = v.reshape(v.shape[:-1] + (-1, 32))
    amax = np.abs(blocks).max(-1, keepdims=True)
    byte = np.maximum(np.where(amax > 0, np.frexp(amax)[1] - 1 + 127, 0) - down, 1)
    scale = np.exp2(byte - 127.0)
    codes = (blocks / scale).astype(np.float32).astype(dtype).astype(np.float64)
    return np.moveaxis((codes * scale).reshape(v.shape), -1, axis)


WIDE = False


def mx_kscale(k):
    if not WIDE:
        return np.ones(k)
    levels = np.array([10, -10, 5, -5, 0])
    if k % 512:
        return np.exp2(np.random.permutation(np.resize(levels, k // 32))).repeat(32)
    a = np.empty((k // 512, 16))
    for p in range(k // 512):
        a[p, :8] = np.random.permutation(np.resize(levels, 8))
        for g in range(8):
            far = levels[np.abs(levels - a[p, g]) >= 10]
            a[p, g + 8] = far[np.random.randint(len(far))]
    return np.exp2(a.ravel()).repeat(32)


BF16 = ml_dtypes.bfloat16


def bf(x):
    return np.asarray(x, np.float32).astype(BF16)


def f64(x):
    return np.asarray(x).astype(np.float64)


E2M1 = np.array([0.0, 0.5, 1.0, 1.5, 2.0, 3.0, 4.0, 6.0, -0.0, -0.5, -1.0, -1.5, -2.0, -3.0, -4.0, -6.0])


def pack_weight(w, fmt):
    k, n = w.shape
    w = f64(bf(w)).reshape(k // 32, 32, n)
    amax = np.abs(w).max(1)
    if fmt == "e4m3":
        byte = np.frexp(amax)[1] - 1 + 127 - 7
    else:
        mant, ex = np.frexp(amax / 6.0)
        byte = np.where(mant > 0.5, ex, ex - 1) + 127
    byte = np.clip(np.where(amax > 0, byte, 1), 1, 254)
    scaled = (w * np.exp2(127.0 - byte)[:, None, :]).reshape(k, n).astype(np.float32)
    by_word = np.ascontiguousarray(scaled.reshape(k // 512, 128, 4, n).transpose(0, 1, 3, 2))
    if fmt == "e4m3":
        words = by_word.astype(ml_dtypes.float8_e4m3fn).view(np.uint8)
    else:
        c = by_word.astype(ml_dtypes.float4_e2m1fn).view(np.uint8) & 0xF
        words = c[..., 0::2] | (c[..., 1::2] << 4)
    return np.ascontiguousarray(words), np.ascontiguousarray(byte.astype(np.uint8).reshape(k // 512, 16, n))


def unpack_weight(words, scales, fmt):
    g, p, n, _ = words.shape
    if fmt == "e4m3":
        vals = np.ascontiguousarray(words).view(ml_dtypes.float8_e4m3fn).astype(np.float64)
    else:
        nib = np.empty((g, p, n, 4), np.uint8)
        nib[..., 0::2] = words & 0xF
        nib[..., 1::2] = words >> 4
        vals = E2M1[nib]
    vals = vals * np.repeat(np.exp2(scales.astype(np.float64) - 127.0), 8, axis=1)[..., None]
    return vals.transpose(0, 1, 3, 2).reshape(g * 512, n)
def pack4(w):
    words, scales = pack_weight(w, "e2m1")
    return words.reshape(words.shape[0], 128, -1), scales


def unpack4(words, scales):
    return unpack_weight(words.reshape(words.shape[0], 128, -1, 2), scales, "e2m1")


def planes(Y):
    n, m = Y.shape
    b = f64(bf(Y)).reshape(n // 32, 32, m)
    amax = np.abs(b).max(1)
    byte = np.clip(np.where(amax > 0, np.frexp(amax)[1] - 1 + 127 - 7, 1), 1, 254)
    codes = (b * np.exp2(127.0 - byte)[:, None, :]).reshape(n, m).astype(np.float32).astype(ml_dtypes.float8_e4m3fn).view(np.uint8)
    words = codes.reshape(n // 512, 128, 4, m).transpose(0, 1, 3, 2)
    return np.ascontiguousarray(words), np.ascontiguousarray(byte.astype(np.uint8).reshape(n // 512, 16, m))


M, K, N = 1536, 1024, 1024
SIGMA = np.sqrt(K)
SPREAD = 0.8


def setup_inputs():
    s = mx_kscale(K)[:, None]
    a = np.sign(np.random.rand(K, N) - 0.5)
    b = np.sign(np.random.rand(K, N) - 0.5)
    sent = np.concatenate([a, b], axis=1)[:, np.random.randint(2 * N, size=M)]
    received = sent + SIGMA * np.random.randn(K, M)
    llr = 2.0 * received / SIGMA ** 2
    X = llr * SIGMA / 2.0
    A = a * 0.5 / SIGMA
    B = b * 0.5 / SIGMA
    W = np.random.randn(K, N) / np.sqrt(K) * np.exp(SPREAD * np.random.randn(1, N))
    x_words, x_scales = pack_weight(X * s, "e4m3")
    a_words, a_scales = pack4(A / s)
    b_words, b_scales = pack_weight(B / s, "e4m3")
    return {"x_words": x_words, "x_scales": x_scales,
            "a_words": a_words, "a_scales": a_scales,
            "b_words": b_words, "b_scales": b_scales,
            "w": bf(W / s), "h": bf(0.3 * np.random.randn(N))}


def reference(x_words, x_scales, a_words, a_scales, b_words, b_scales, w, h):
    X = unpack_weight(x_words, x_scales, "e4m3")
    P = X.T @ unpack4(a_words, a_scales)
    Q = X.T @ unpack_weight(b_words, b_scales, "e4m3")
    R = X.T @ mxq(f64(w), 0, "e4m3")
    y = np.tanh(P - Q + f64(h)) * R
    words, scales = planes(y.T)
    return y, words, scales

@@ -1,0 +1,339 @@
+from contextlib import ExitStack
+
+import concourse.mybir as mybir
+from concourse.masks import make_identity
+
+M, K, N = 1536, 1024, 1024
+FLOPS = 3 * 2 * M * K * N
+
+F32 = mybir.dt.float32
+BF16 = mybir.dt.bfloat16
+I32 = mybir.dt.int32
+U32 = mybir.dt.uint32
+U8 = mybir.dt.uint8
+FP8X4 = mybir.dt.float8_e4m3fn_x4
+FP4X4 = mybir.dt.float4_e2m1fn_x4
+ALU = mybir.AluOpType
+ACT = mybir.ActivationFunctionType
+
+P = 128
+PASSES = K // 512
+HALF = 512
+ROW_TILES = M // P
+UNITS = 2 * ROW_TILES
+X_CHUNKS = ((0, 256), (256, 640), (640, 1536))
+XS_CHUNKS = ((0, 768), (768, 1536))
+LEAD = 4
+LAG = 2
+GROUPS = tuple((u, 2) for u in range(0, 22, 2)) + ((22, 1), (23, 1))
+
+
+def tile_codeword_pair_posterior_readout_k3_kernel(
+    tc, x_words, x_scales, a_words, a_scales, b_words, b_scales, w, h, out_0, out_1, out_2
+):
+    nc = tc.nc
+    with ExitStack() as ctx:
+        keep = ctx.enter_context(tc.tile_pool(name="keep", bufs=1))
+        work = ctx.enter_context(tc.tile_pool(name="work", bufs=4))
+        psum = ctx.enter_context(tc.psum_pool(name="psum", bufs=1))
+        ctx.enter_context(tc.manual_schedule())
+
+        x_src = x_words.rearrange("g p m t -> p g (m t)")
+        b_src = b_words.rearrange("g p n t -> p g (n t)")
+        a_src = a_words.rearrange("g p c -> p g c")
+
+        xc = [keep.tile([P, PASSES, hi - lo], U32, name="xc%d" % i, align_bytes=64) for i, (lo, hi) in enumerate(X_CHUNKS)]
+        xs = [keep.tile([P, PASSES, hi - lo], U8, name="xs%d" % i, align_bytes=64) for i, (lo, hi) in enumerate(XS_CHUNKS)]
+        ac = [keep.tile([P, PASSES, 2 * HALF], U8, name="ac%d" % f, align_bytes=64) for f in range(2)]
+        asc = [keep.tile([P, PASSES, HALF], U8, name="as%d" % f, align_bytes=64) for f in range(2)]
+        bc = [[keep.tile([P, HALF], U32, name="bc%d%d" % (f, g), align_bytes=64) for g in range(PASSES)] for f in range(2)]
+        bsc = [keep.tile([P, HALF], U8, name="bs%d" % f, align_bytes=64) for f in range(2)]
+        wraw = [[keep.tile([P, 4, HALF], BF16, name="wr%d%d" % (f, g), align_bytes=64) for g in range(PASSES)] for f in range(2)]
+        wgrp = [[keep.tile([P, 4 * HALF], BF16, name="wg%d%d" % (f, g), align_bytes=64) for g in range(PASSES)] for f in range(2)]
+        wc = [[keep.tile([P, HALF], U32, name="wc%d%d" % (f, g), align_bytes=64) for g in range(PASSES)] for f in range(2)]
+        wsc = [[keep.tile([P, HALF], U8, name="ws%d%d" % (f, g), align_bytes=64) for g in range(PASSES)] for f in range(2)]
+        ysc = [keep.tile([P, M], U8, name="ys%d" % f, align_bytes=64) for f in range(2)]
+        h_rows = keep.tile([P, N // P], BF16, name="h_rows", align_bytes=64)
+        h_all = keep.tile([P, N], BF16, name="h_all", align_bytes=64)
+        ident = keep.tile([P, P], F32, name="ident", align_bytes=64)
+
+        def load_x(eng, i):
+            lo, hi = X_CHUNKS[i]
+            eng.dma_start(out=xc[i][:].bitcast(I32), in_=x_src[:, :, 4 * lo : 4 * hi].bitcast(I32))
+
+        def load_plane(eng, plane, src, lo, hi, quadrants):
+            for q in quadrants:
+                eng.dma_start(
+                    out=plane[32 * q : 32 * q + 4, :, :].bitcast(I32),
+                    in_=src[:, 4 * q : 4 * q + 4, lo:hi].rearrange("g r n -> r g n").bitcast(I32),
+                )
+
+        def load_b_plane(eng, f, quadrants):
+            for q in quadrants:
+                eng.dma_start(
+                    out=bsc[f][32 * q + 4 : 32 * q + 12, :].bitcast(I32),
+                    in_=b_scales[:, 4 * q : 4 * q + 4, f * HALF : (f + 1) * HALF].bitcast(I32),
+                )
+
+        def load_b(eng, f, g):
+            eng.dma_start(out=bc[f][g][:].bitcast(I32), in_=b_src[:, g, 4 * f * HALF : 4 * (f + 1) * HALF].bitcast(I32))
+
+        def load_a(eng, f):
+            eng.dma_start(out=ac[f][:].bitcast(I32), in_=a_src[:, :, 2 * f * HALF : 2 * (f + 1) * HALF].bitcast(I32))
+
+        def load_w(eng, f, g):
+            eng.dma_start(
+                out=wraw[f][g][:],
+                in_=w[512 * g : 512 * (g + 1), f * HALF : (f + 1) * HALF].rearrange("(p j) n -> p j n", j=4),
+            )
+
+        def zero(plane):
+            nc.vector.memset(plane[:].bitcast(I32), 0)
+
+        zero(xs[0])
+        zero(bsc[0])
+        zero(asc[0])
+        make_identity(nc, ident[:])
+
+        nc.scalar.dma_start(out=h_rows[:], in_=h.rearrange("(p j) -> p j", p=P))
+        load_plane(nc.sync, xs[0], x_scales, 0, 768, range(4))
+        load_b_plane(nc.sync, 0, range(0, 1))
+        load_x(nc.sync, 0)
+        load_b(nc.sync, 0, 0)
+        load_b_plane(nc.sync, 0, range(1, 4))
+        load_b(nc.sync, 0, 1)
+        load_a(nc.sync, 0)
+        load_plane(nc.sync, asc[0], a_scales, 0, HALF, range(0, 1))
+        load_w(nc.sync, 0, 0)
+        load_plane(nc.sync, asc[0], a_scales, 0, HALF, range(1, 4))
+        load_x(nc.sync, 1)
+        load_w(nc.sync, 0, 1)
+        zero(xs[1])
+        zero(bsc[1])
+        zero(asc[1])
+        load_plane(nc.sync, xs[1], x_scales, 768, M, range(4))
+        load_x(nc.sync, 2)
+        load_w(nc.sync, 1, 0)
+        load_w(nc.sync, 1, 1)
+        load_plane(nc.sync, asc[1], a_scales, HALF, N, range(4))
+        load_b_plane(nc.sync, 1, range(4))
+        load_b(nc.sync, 1, 0)
+        load_b(nc.sync, 1, 1)
+        load_a(nc.sync, 1)
+
+        def spread_h():
+            bank = psum.tile([P, 4, P], F32, name="turned", tag="turned", bufs=2)
+            words = h_rows[:].bitcast(F32)
+            for j in range(4):
+                nc.tensor.transpose(bank[:, j, :], words[:, j : j + 1].to_broadcast([P, P]), ident[:])
+            nc.scalar.copy(
+                out=h_all[:].bitcast(F32).rearrange("m (p j) -> m p j", j=4),
+                in_=bank[:].rearrange("m j p -> m p j"),
+            )
+
+        def w_views(f, g, lo, hi):
+            return (
+                wgrp[f][g][:, 4 * lo : 4 * hi].rearrange("p (c i t) -> p c t i", i=4, t=4),
+                wraw[f][g][:, :, lo:hi].rearrange("p t (c i) -> p c t i", i=4),
+            )
+
+        def group_w_scalar(f, g, lo, hi):
+            dst, src = w_views(f, g, lo, hi)
+            nc.scalar.activation(out=dst, in_=src, func=ACT.Copy)
+
+        def group_w_gpsimd(f, g, lo, hi):
+            dst, src = w_views(f, g, lo, hi)
+            nc.gpsimd.tensor_scalar(out=dst, in0=src, scalar1=1.0, scalar2=0.0, op0=ALU.mult, op1=ALU.add)
+
+        def group_w_vector(f, g, lo, hi):
+            dst, src = w_views(f, g, lo, hi)
+            nc.vector.tensor_copy(out=dst, in_=src)
+
+        def quantize_w(f, g):
+            nc.vector.quantize_mx(out=wc[f][g][:].bitcast(FP8X4), scales=wsc[f][g][:], in_=wgrp[f][g][:])
+
+        def x_operand(u, g):
+            m0 = (u % ROW_TILES) * P
+            i = [lo <= m0 < hi for lo, hi in X_CHUNKS].index(True)
+            j = [lo <= m0 < hi for lo, hi in XS_CHUNKS].index(True)
+            c0 = m0 - X_CHUNKS[i][0]
+            s0 = m0 - XS_CHUNKS[j][0]
+            return xc[i][:, g, c0 : c0 + P].bitcast(FP8X4), xs[j][:, g, s0 : s0 + P]
+
+        def product(u, moving):
+            bank = psum.tile([P, HALF], F32, name="acc", tag="acc", bufs=6)
+            for g in range(PASSES):
+                codes, scales = x_operand(u, g)
+                rhs, rhs_scale = moving(u // ROW_TILES, g)
+                nc.tensor.matmul_mx(
+                    out=bank[:], lhsT=codes, lhsT_scale=scales, rhs=rhs, rhs_scale=rhs_scale,
+                    start=(g == 0), stop=(g == PASSES - 1),
+                )
+            return bank
+
+        def a_operand(f, g):
+            return ac[f][:, g, :].bitcast(FP4X4), asc[f][:, g, :]
+
+        def b_operand(f, g):
+            return bc[f][g][:].bitcast(FP8X4), bsc[f][4 + 4 * g :, :]
+
+        def w_operand(f, g):
+            return wc[f][g][:].bitcast(FP8X4), wsc[f][g][:]
+
+        shifted, metric, mean, y, rounded, grouped = {}, {}, {}, {}, {}, {}
+
+        def do_q(u):
+            f = u // ROW_TILES
+            bank = product(u, b_operand)
+            shifted[u] = work.tile([P, HALF], F32, name="shifted", bufs=3)
+            nc.vector.tensor_tensor(out=shifted[u][:], in0=h_all[:, f * HALF : (f + 1) * HALF], in1=bank[:], op=ALU.subtract)
+
+        def do_p(u):
+            bank = product(u, a_operand)
+            metric[u] = work.tile([P, HALF], F32, name="metric", bufs=8)
+            nc.vector.tensor_tensor(out=metric[u][:], in0=bank[:], in1=shifted[u][:], op=ALU.add)
+
+        def do_tanh(u):
+            mean[u] = work.tile([P, HALF], F32, name="mean", bufs=8)
+            nc.scalar.activation(out=mean[u][:], in_=metric[u][:], func=ACT.Tanh)
+
+        def do_r(u, direct=False):
+            f, mt = divmod(u, ROW_TILES)
+            bank = product(u, w_operand)
+            if direct:
+                rounded[u] = work.tile([P, HALF], BF16, name="rounded", bufs=8, align_bytes=64)
+                nc.vector.tensor_tensor(
+                    out=rounded[u][:].rearrange("m (v p e) -> m v p e", v=2, e=2),
+                    in0=bank[:].rearrange("m (p v e) -> m v p e", v=2, e=2),
+                    in1=mean[u][:].rearrange("m (p v e) -> m v p e", v=2, e=2),
+                    op=ALU.mult,
+                )
+            y[u] = work.tile([P, HALF], F32, name="y", bufs=8)
+            nc.vector.tensor_tensor(out=y[u][:], in0=bank[:], in1=mean[u][:], op=ALU.mult)
+            nc.sync.dma_start(out=out_0[mt * P : (mt + 1) * P, f * HALF : (f + 1) * HALF], in_=y[u][:])
+
+        def do_round(u):
+            rounded[u] = work.tile([P, HALF], BF16, name="rounded", bufs=8, align_bytes=64)
+            nc.scalar.copy(
+                out=rounded[u][:].rearrange("m (v p e) -> m v p e", v=2, e=2),
+                in_=y[u][:].rearrange("m (p v e) -> m v p e", v=2, e=2),
+            )
+
+        turned = {}
+
+        def do_turn(i):
+            u0, count = GROUPS[i]
+            turned[i] = psum.tile([P, 4, P], F32, name="turned", tag="turned", bufs=2)
+            for j in range(count):
+                words = rounded[u0 + j][:].bitcast(F32)
+                for v in range(2):
+                    nc.tensor.transpose(turned[i][:, 2 * j + v, :], words[:, v * P : (v + 1) * P], ident[:])
+
+        def do_group(i):
+            u0, count = GROUPS[i]
+            grouped[i] = work.tile([P, 2 * HALF], BF16, name="grouped", bufs=3, align_bytes=64)
+            nc.scalar.copy(
+                out=grouped[i][:].bitcast(F32)[:, 0 : 2 * P * count].rearrange("p (j m v) -> p j m v", j=count, v=2),
+                in_=turned[i][:, 0 : 2 * count, :].rearrange("p (j v) m -> p j m v", v=2),
+            )
+
+        pair_codes = {}
+
+        def do_planes(i):
+            u0, count = GROUPS[i]
+            f, mt = divmod(u0, ROW_TILES)
+            if u0 % 2 == 0:
+                pair_codes[u0 // 2] = work.tile([P, 2 * P], U32, name="codes", bufs=6, align_bytes=64)
+            codes = pair_codes[u0 // 2]
+            c0 = (u0 % 2) * P
+            nc.vector.quantize_mx(
+                out=codes[:, c0 : c0 + count * P].bitcast(FP8X4),
+                scales=ysc[f][:, mt * P : (mt + count) * P],
+                in_=grouped[i][:, 0 : 4 * count * P],
+            )
+            if (u0 + count) % 2 == 0:
+                m1 = (mt + count) * P
+                nc.sync.dma_start(
+                    out=out_1[f].rearrange("p m t -> p (m t)")[:, 4 * (m1 - 2 * P) : 4 * m1].bitcast(I32),
+                    in_=codes[:].bitcast(I32),
+                )
+
+        def store_scales(f, m0, m1, engines):
+            for q in range(4):
+                engines[q].dma_start(
+                    out=out_2[f, 4 * q : 4 * q + 4, m0:m1].bitcast(I32),
+                    in_=ysc[f][32 * q : 32 * q + 4, m0:m1].bitcast(I32),
+                )
+
+        spread_h()
+        for g in range(PASSES):
+            group_w_scalar(0, g, 0, HALF // 2)
+            group_w_gpsimd(0, g, 2 * P, 3 * P)
+            group_w_gpsimd(0, g, 3 * P, 4 * P)
+        do_q(0)
+        do_q(1)
+        do_p(0)
+        do_q(2)
+        quantize_w(0, 0)
+        do_p(1)
+        do_tanh(0)
+        do_tanh(1)
+        do_q(3)
+        do_p(2)
+        quantize_w(0, 1)
+        do_p(3)
+        do_tanh(2)
+        do_tanh(3)
+        for g in range(PASSES):
+            for lo in range(0, HALF, P):
+                group_w_gpsimd(1, g, lo, lo + P)
+
+        turn_at = {7: (0, 1), 11: (2, 3), 15: (4, 5), 19: (6, 7), 22: (8,), 23: (9,)}
+        group_at, planes_at = {}, {}
+        for s, run in turn_at.items():
+            for late, i in enumerate(run):
+                group_at[s + late] = i
+                planes_at[s + late + 1] = i
+        next_r = 0
+        for s in range(LEAD, UNITS):
+            do_q(s)
+            for i in turn_at.get(s, ()):
+                do_turn(i)
+            if s == UNITS - 1:
+                do_group(group_at[s])
+            done = [next_r]
+            do_r(next_r)
+            next_r = next_r + 1
+            do_p(s)
+            if s - next_r >= LAG:
+                done.append(next_r)
+                do_r(next_r)
+                next_r = next_r + 1
+            for u in done:
+                do_round(u)
+            do_tanh(s)
+            if s in group_at and s < UNITS - 1:
+                do_group(group_at[s])
+            if s in planes_at:
+                do_planes(planes_at[s])
+                if planes_at[s] == 5:
+                    store_scales(0, 0, M, [nc.sync] * 4)
+                if planes_at[s] == 8:
+                    store_scales(1, 0, 768, [nc.sync] * 4)
+            if s in (9, 10):
+                quantize_w(1, s - 9)
+
+        do_r(22)
+        do_planes(9)
+        do_round(22)
+        do_r(23, direct=True)
+        do_turn(10)
+        do_turn(11)
+        do_group(10)
+        do_turn(12)
+        do_group(11)
+        do_group(12)
+        do_planes(10)
+        do_planes(11)
+        do_planes(12)
+        store_scales(1, 768, M, [nc.sync, nc.scalar, nc.sync, nc.scalar])

@@ -142,7 +142,8 @@ def tile_codeword_pair_posterior_readout_k3_kernel(
             nc.scalar.activation(out=dst, in_=src, func=ACT.Copy)
 
         def group_w_gpsimd(f, g, lo, hi):
-            dst, src = w_views(f, g, lo, hi)
+            dst = wgrp[f][g][:, 4 * lo : 4 * hi].rearrange("p (c t) -> p c t", t=4)
+            src = wraw[f][g][:, :, lo:hi].rearrange("p t c -> p c t")
             nc.gpsimd.tensor_scalar(out=dst, in0=src, scalar1=1.0, scalar2=0.0, op0=ALU.mult, op1=ALU.add)
 
         def group_w_vector(f, g, lo, hi):
@@ -212,6 +213,23 @@ def tile_codeword_pair_posterior_readout_k3_kernel(
             nc.vector.tensor_tensor(out=y[u][:], in0=bank[:], in1=mean[u][:], op=ALU.mult)
             nc.sync.dma_start(out=out_0[mt * P : (mt + 1) * P, f * HALF : (f + 1) * HALF], in_=y[u][:])
 
+        def do_r_aside(u):
+            f, mt = divmod(u, ROW_TILES)
+            bank = product(u, w_operand)
+            readout = work.tile([P, HALF], F32, name="readout", bufs=2)
+            nc.scalar.copy(out=readout[:], in_=bank[:])
+            y[u] = work.tile([P, HALF], F32, name="y", bufs=8)
+            for lo in range(0, HALF, HALF // 2):
+                cols = slice(lo, lo + HALF // 2)
+                nc.gpsimd.tensor_tensor(out=y[u][:, cols], in0=readout[:, cols], in1=mean[u][:, cols], op=ALU.mult)
+            nc.sync.dma_start(out=out_0[mt * P : (mt + 1) * P, f * HALF : (f + 1) * HALF], in_=y[u][:])
+            rounded[u] = work.tile([P, HALF], BF16, name="rounded", bufs=8, align_bytes=64)
+            nc.gpsimd.tensor_scalar(
+                out=rounded[u][:].rearrange("m (v p e) -> m v p e", v=2, e=2),
+                in0=y[u][:].rearrange("m (p v e) -> m v p e", v=2, e=2),
+                scalar1=1.0, scalar2=0.0, op0=ALU.mult, op1=ALU.add,
+            )
+
         def do_round(u):
             rounded[u] = work.tile([P, HALF], BF16, name="rounded", bufs=8, align_bytes=64)
             nc.scalar.copy(
@@ -223,7 +241,10 @@ def tile_codeword_pair_posterior_readout_k3_kernel(
 
         def do_turn(i):
             u0, count = GROUPS[i]
-            turned[i] = psum.tile([P, 4, P], F32, name="turned", tag="turned", bufs=2)
+            if i == len(GROUPS) - 1:
+                turned[i] = psum.tile([P, 4, P], F32, name="acc", tag="acc", bufs=6)
+            else:
+                turned[i] = psum.tile([P, 4, P], F32, name="turned", tag="turned", bufs=2)
             for j in range(count):
                 words = rounded[u0 + j][:].bitcast(F32)
                 for v in range(2):
@@ -273,14 +294,14 @@ def tile_codeword_pair_posterior_readout_k3_kernel(
         do_q(0)
         do_q(1)
         do_p(0)
-        do_q(2)
         quantize_w(0, 0)
+        do_q(2)
         do_p(1)
         do_tanh(0)
         do_tanh(1)
         do_q(3)
-        do_p(2)
         quantize_w(0, 1)
+        do_p(2)
         do_p(3)
         do_tanh(2)
         do_tanh(3)
@@ -288,21 +309,32 @@ def tile_codeword_pair_posterior_readout_k3_kernel(
             for lo in range(0, HALF, P):
                 group_w_gpsimd(1, g, lo, lo + P)
 
-        turn_at = {7: (0, 1), 11: (2, 3), 15: (4, 5), 19: (6, 7), 22: (8,), 23: (9,)}
+        turn_at = {7: (0, 1), 11: (2, 3), 15: (4, 5), 19: (6, 7), 21: (8,), 23: (9,)}
         group_at, planes_at = {}, {}
         for s, run in turn_at.items():
             for late, i in enumerate(run):
                 group_at[s + late] = i
-                planes_at[s + late + 1] = i
+                if i < 8:
+                    planes_at[s + 2 * late + 1] = i
         next_r = 0
         for s in range(LEAD, UNITS):
             do_q(s)
             for i in turn_at.get(s, ()):
                 do_turn(i)
-            if s == UNITS - 1:
+            if s in group_at:
                 do_group(group_at[s])
-            done = [next_r]
-            do_r(next_r)
+            done = []
+            if s >= 8 and s % 2 == 0:
+                do_planes(planes_at[s])
+                if s == UNITS - 2:
+                    do_planes(8)
+                    store_scales(1, 0, 768, [nc.sync] * 4)
+                do_r_aside(next_r)
+                if planes_at[s] == 5:
+                    store_scales(0, 0, M, [nc.sync] * 4)
+            else:
+                done.append(next_r)
+                do_r(next_r)
             next_r = next_r + 1
             do_p(s)
             if s - next_r >= LAG:
@@ -312,16 +344,8 @@ def tile_codeword_pair_posterior_readout_k3_kernel(
             for u in done:
                 do_round(u)
             do_tanh(s)
-            if s in group_at and s < UNITS - 1:
-                do_group(group_at[s])
-            if s in planes_at:
-                do_planes(planes_at[s])
-                if planes_at[s] == 5:
-                    store_scales(0, 0, M, [nc.sync] * 4)
-                if planes_at[s] == 8:
-                    store_scales(1, 0, 768, [nc.sync] * 4)
-            if s in (9, 10):
-                quantize_w(1, s - 9)
+            if s in (9, 11):
+                quantize_w(1, (s - 9) // 2)
 
         do_r(22)
         do_planes(9)

@@ -21,7 +21,7 @@ PASSES = K // 512
 HALF = 512
 ROW_TILES = M // P
 UNITS = 2 * ROW_TILES
-X_CHUNKS = ((0, 256), (256, 640), (640, 1536))
+X_CHUNKS = ((0, 384), (384, 768), (768, 1536))
 XS_CHUNKS = ((0, 768), (768, 1536))
 LEAD = 4
 LAG = 2
@@ -106,8 +106,8 @@ def tile_codeword_pair_posterior_readout_k3_kernel(
         load_plane(nc.sync, asc[0], a_scales, 0, HALF, range(0, 1))
         load_w(nc.sync, 0, 0)
         load_plane(nc.sync, asc[0], a_scales, 0, HALF, range(1, 4))
-        load_x(nc.sync, 1)
         load_w(nc.sync, 0, 1)
+        load_x(nc.sync, 1)
         zero(xs[1])
         zero(bsc[1])
         zero(asc[1])
@@ -213,7 +213,7 @@ def tile_codeword_pair_posterior_readout_k3_kernel(
             nc.vector.tensor_tensor(out=y[u][:], in0=bank[:], in1=mean[u][:], op=ALU.mult)
             nc.sync.dma_start(out=out_0[mt * P : (mt + 1) * P, f * HALF : (f + 1) * HALF], in_=y[u][:])
 
-        def do_r_aside(u):
+        def do_r_aside(u, round_here):
             f, mt = divmod(u, ROW_TILES)
             bank = product(u, w_operand)
             readout = work.tile([P, HALF], F32, name="readout", bufs=2)
@@ -223,12 +223,13 @@ def tile_codeword_pair_posterior_readout_k3_kernel(
                 cols = slice(lo, lo + HALF // 2)
                 nc.gpsimd.tensor_tensor(out=y[u][:, cols], in0=readout[:, cols], in1=mean[u][:, cols], op=ALU.mult)
             nc.sync.dma_start(out=out_0[mt * P : (mt + 1) * P, f * HALF : (f + 1) * HALF], in_=y[u][:])
-            rounded[u] = work.tile([P, HALF], BF16, name="rounded", bufs=8, align_bytes=64)
-            nc.gpsimd.tensor_scalar(
-                out=rounded[u][:].rearrange("m (v p e) -> m v p e", v=2, e=2),
-                in0=y[u][:].rearrange("m (p v e) -> m v p e", v=2, e=2),
-                scalar1=1.0, scalar2=0.0, op0=ALU.mult, op1=ALU.add,
-            )
+            if round_here:
+                rounded[u] = work.tile([P, HALF], BF16, name="rounded", bufs=8, align_bytes=64)
+                nc.gpsimd.tensor_scalar(
+                    out=rounded[u][:].rearrange("m (v p e) -> m v p e", v=2, e=2),
+                    in0=y[u][:].rearrange("m (p v e) -> m v p e", v=2, e=2),
+                    scalar1=1.0, scalar2=0.0, op0=ALU.mult, op1=ALU.add,
+                )
 
         def do_round(u):
             rounded[u] = work.tile([P, HALF], BF16, name="rounded", bufs=8, align_bytes=64)
@@ -250,34 +251,36 @@ def tile_codeword_pair_posterior_readout_k3_kernel(
                 for v in range(2):
                     nc.tensor.transpose(turned[i][:, 2 * j + v, :], words[:, v * P : (v + 1) * P], ident[:])
 
+        quad_codes = {}
+
         def do_group(i):
             u0, count = GROUPS[i]
-            grouped[i] = work.tile([P, 2 * HALF], BF16, name="grouped", bufs=3, align_bytes=64)
+            if u0 % 4 == 0:
+                grouped[u0 // 4] = work.tile([P, 4 * HALF], BF16, name="grouped", bufs=2, align_bytes=64)
+            w0 = 2 * P * (u0 % 4)
             nc.scalar.copy(
-                out=grouped[i][:].bitcast(F32)[:, 0 : 2 * P * count].rearrange("p (j m v) -> p j m v", j=count, v=2),
+                out=grouped[u0 // 4][:].bitcast(F32)[:, w0 : w0 + 2 * P * count].rearrange("p (j m v) -> p j m v", j=count, v=2),
                 in_=turned[i][:, 0 : 2 * count, :].rearrange("p (j v) m -> p j m v", v=2),
             )
 
-        pair_codes = {}
-
-        def do_planes(i):
-            u0, count = GROUPS[i]
+        def do_planes(u0, count):
             f, mt = divmod(u0, ROW_TILES)
-            if u0 % 2 == 0:
-                pair_codes[u0 // 2] = work.tile([P, 2 * P], U32, name="codes", bufs=6, align_bytes=64)
-            codes = pair_codes[u0 // 2]
-            c0 = (u0 % 2) * P
+            if u0 % 4 == 0:
+                quad_codes[u0 // 4] = work.tile([P, HALF], U32, name="codes", bufs=3, align_bytes=64)
+            c0 = (u0 % 4) * P
             nc.vector.quantize_mx(
-                out=codes[:, c0 : c0 + count * P].bitcast(FP8X4),
+                out=quad_codes[u0 // 4][:, c0 : c0 + count * P].bitcast(FP8X4),
                 scales=ysc[f][:, mt * P : (mt + count) * P],
-                in_=grouped[i][:, 0 : 4 * count * P],
+                in_=grouped[u0 // 4][:, 4 * c0 : 4 * (c0 + count * P)],
             )
-            if (u0 + count) % 2 == 0:
-                m1 = (mt + count) * P
-                nc.sync.dma_start(
-                    out=out_1[f].rearrange("p m t -> p (m t)")[:, 4 * (m1 - 2 * P) : 4 * m1].bitcast(I32),
-                    in_=codes[:].bitcast(I32),
-                )
+
+        def store_codes(u0, count):
+            f, mt = divmod(u0, ROW_TILES)
+            c0 = (u0 % 4) * P
+            nc.sync.dma_start(
+                out=out_1[f].rearrange("p m t -> p (m t)")[:, 4 * mt * P : 4 * (mt + count) * P].bitcast(I32),
+                in_=quad_codes[u0 // 4][:, c0 : c0 + count * P].bitcast(I32),
+            )
 
         def store_scales(f, m0, m1, engines):
             for q in range(4):
@@ -287,68 +290,80 @@ def tile_codeword_pair_posterior_readout_k3_kernel(
                 )
 
         spread_h()
-        for g in range(PASSES):
-            group_w_scalar(0, g, 0, HALF // 2)
-            group_w_gpsimd(0, g, 2 * P, 3 * P)
-            group_w_gpsimd(0, g, 3 * P, 4 * P)
+        group_w_scalar(0, 0, 0, HALF // 2)
+        group_w_scalar(0, 1, 0, HALF)
         do_q(0)
         do_q(1)
         do_p(0)
-        quantize_w(0, 0)
+        group_w_vector(0, 0, HALF // 2, HALF)
         do_q(2)
+        quantize_w(0, 0)
         do_p(1)
-        do_tanh(0)
-        do_tanh(1)
-        do_q(3)
         quantize_w(0, 1)
+        do_q(3)
         do_p(2)
+        do_q(4)
         do_p(3)
-        do_tanh(2)
-        do_tanh(3)
+        for u in range(4):
+            do_tanh(u)
         for g in range(PASSES):
             for lo in range(0, HALF, P):
                 group_w_gpsimd(1, g, lo, lo + P)
-
-        turn_at = {7: (0, 1), 11: (2, 3), 15: (4, 5), 19: (6, 7), 21: (8,), 23: (9,)}
-        group_at, planes_at = {}, {}
+        do_r(0)
+        do_p(4)
+        do_r(1)
+        do_round(0)
+        do_round(1)
+        do_tanh(4)
+        aside = {8: True, 9: True, 12: True, 13: True, 16: True}
+        late_round = {}
+        turn_at = {8: (0, 1), 11: (2, 3), 15: (4, 5), 19: (6, 7), 21: (8,), 23: (9,)}
+        group_at = {}
         for s, run in turn_at.items():
             for late, i in enumerate(run):
                 group_at[s + late] = i
-                if i < 8:
-                    planes_at[s + 2 * late + 1] = i
-        next_r = 0
-        for s in range(LEAD, UNITS):
+        planes_at = {10: (0, 4), 14: (4, 4), 18: (8, 4), 21: (12, 4)}
+        w_at = {}
+        wq_at = {8: 0, 9: 1}
+        next_r = 2
+        for s in range(5, UNITS):
             do_q(s)
             for i in turn_at.get(s, ()):
                 do_turn(i)
             if s in group_at:
                 do_group(group_at[s])
-            done = []
-            if s >= 8 and s % 2 == 0:
-                do_planes(planes_at[s])
-                if s == UNITS - 2:
-                    do_planes(8)
-                    store_scales(1, 0, 768, [nc.sync] * 4)
-                do_r_aside(next_r)
-                if planes_at[s] == 5:
+            done = late_round.get(s, [])
+            if s in planes_at:
+                do_planes(*planes_at[s])
+                store_codes(*planes_at[s])
+                if planes_at[s][0] + planes_at[s][1] == 12:
                     store_scales(0, 0, M, [nc.sync] * 4)
-            else:
-                done.append(next_r)
-                do_r(next_r)
-            next_r = next_r + 1
-            do_p(s)
-            if s - next_r >= LAG:
-                done.append(next_r)
-                do_r(next_r)
-                next_r = next_r + 1
+            for slot in range(2):
+                if slot == 0 or s - next_r >= LAG:
+                    if next_r in aside:
+                        do_r_aside(next_r, aside[next_r])
+                        if not aside[next_r]:
+                            late_round[s + 1] = late_round.get(s + 1, []) + [next_r]
+                    else:
+                        done.append(next_r)
+                        do_r(next_r)
+                    next_r = next_r + 1
+                if slot == 0:
+                    do_p(s)
             for u in done:
                 do_round(u)
             do_tanh(s)
-            if s in (9, 11):
-                quantize_w(1, (s - 9) // 2)
-
+            for fn, g, piece in w_at.get(s, ()):
+                fn(1, g, piece * P, (piece + 1) * P)
+            if s in wq_at:
+                quantize_w(1, wq_at[s])
+            if s == 22:
+                do_planes(16, 2)
+                store_codes(16, 2)
+                store_scales(1, 0, 768, [nc.sync] * 4)
         do_r(22)
-        do_planes(9)
+        do_planes(18, 2)
+        store_codes(18, 2)
         do_round(22)
         do_r(23, direct=True)
         do_turn(10)
@@ -357,7 +372,8 @@ def tile_codeword_pair_posterior_readout_k3_kernel(
         do_turn(12)
         do_group(11)
         do_group(12)
-        do_planes(10)
-        do_planes(11)
-        do_planes(12)
+        do_planes(20, 2)
+        do_planes(22, 1)
+        do_planes(23, 1)
+        store_codes(20, 4)
         store_scales(1, 768, M, [nc.sync, nc.scalar, nc.sync, nc.scalar])

from contextlib import ExitStack

import concourse.mybir as mybir
from concourse.masks import make_identity

M, K, N = 1536, 1024, 1024
FLOPS = 3 * 2 * M * K * N

F32 = mybir.dt.float32
BF16 = mybir.dt.bfloat16
I32 = mybir.dt.int32
U32 = mybir.dt.uint32
U8 = mybir.dt.uint8
FP8X4 = mybir.dt.float8_e4m3fn_x4
FP4X4 = mybir.dt.float4_e2m1fn_x4
ALU = mybir.AluOpType
ACT = mybir.ActivationFunctionType

P = 128
PASSES = K // 512
HALF = 512
ROW_TILES = M // P
UNITS = 2 * ROW_TILES
X_CHUNKS = ((0, 384), (384, 768), (768, 1536))
XS_CHUNKS = ((0, 768), (768, 1536))
LEAD = 4
LAG = 2
GROUPS = tuple((u, 2) for u in range(0, 22, 2)) + ((22, 1), (23, 1))


def tile_codeword_pair_posterior_readout_k3_kernel(
    tc, x_words, x_scales, a_words, a_scales, b_words, b_scales, w, h, out_0, out_1, out_2
):
    nc = tc.nc
    with ExitStack() as ctx:
        keep = ctx.enter_context(tc.tile_pool(name="keep", bufs=1))
        work = ctx.enter_context(tc.tile_pool(name="work", bufs=4))
        psum = ctx.enter_context(tc.psum_pool(name="psum", bufs=1))
        ctx.enter_context(tc.manual_schedule())

        x_src = x_words.rearrange("g p m t -> p g (m t)")
        b_src = b_words.rearrange("g p n t -> p g (n t)")
        a_src = a_words.rearrange("g p c -> p g c")

        xc = [keep.tile([P, PASSES, hi - lo], U32, name="xc%d" % i, align_bytes=64) for i, (lo, hi) in enumerate(X_CHUNKS)]
        xs = [keep.tile([P, PASSES, hi - lo], U8, name="xs%d" % i, align_bytes=64) for i, (lo, hi) in enumerate(XS_CHUNKS)]
        ac = [keep.tile([P, PASSES, 2 * HALF], U8, name="ac%d" % f, align_bytes=64) for f in range(2)]
        asc = [keep.tile([P, PASSES, HALF], U8, name="as%d" % f, align_bytes=64) for f in range(2)]
        bc = [[keep.tile([P, HALF], U32, name="bc%d%d" % (f, g), align_bytes=64) for g in range(PASSES)] for f in range(2)]
        bsc = [keep.tile([P, HALF], U8, name="bs%d" % f, align_bytes=64) for f in range(2)]
        wraw = [[keep.tile([P, 4, HALF], BF16, name="wr%d%d" % (f, g), align_bytes=64) for g in range(PASSES)] for f in range(2)]
        wgrp = [[keep.tile([P, 4 * HALF], BF16, name="wg%d%d" % (f, g), align_bytes=64) for g in range(PASSES)] for f in range(2)]
        wc = [[keep.tile([P, HALF], U32, name="wc%d%d" % (f, g), align_bytes=64) for g in range(PASSES)] for f in range(2)]
        wsc = [[keep.tile([P, HALF], U8, name="ws%d%d" % (f, g), align_bytes=64) for g in range(PASSES)] for f in range(2)]
        ysc = [keep.tile([P, M], U8, name="ys%d" % f, align_bytes=64) for f in range(2)]
        h_rows = keep.tile([P, N // P], BF16, name="h_rows", align_bytes=64)
        h_all = keep.tile([P, N], BF16, name="h_all", align_bytes=64)
        ident = keep.tile([P, P], F32, name="ident", align_bytes=64)

        def load_x(eng, i):
            lo, hi = X_CHUNKS[i]
            eng.dma_start(out=xc[i][:].bitcast(I32), in_=x_src[:, :, 4 * lo : 4 * hi].bitcast(I32))

        def load_plane(eng, plane, src, lo, hi, quadrants):
            for q in quadrants:
                eng.dma_start(
                    out=plane[32 * q : 32 * q + 4, :, :].bitcast(I32),
                    in_=src[:, 4 * q : 4 * q + 4, lo:hi].rearrange("g r n -> r g n").bitcast(I32),
                )

        def load_b_plane(eng, f, quadrants):
            for q in quadrants:
                eng.dma_start(
                    out=bsc[f][32 * q + 4 : 32 * q + 12, :].bitcast(I32),
                    in_=b_scales[:, 4 * q : 4 * q + 4, f * HALF : (f + 1) * HALF].bitcast(I32),
                )

        def load_b(eng, f, g):
            eng.dma_start(out=bc[f][g][:].bitcast(I32), in_=b_src[:, g, 4 * f * HALF : 4 * (f + 1) * HALF].bitcast(I32))

        def load_a(eng, f):
            eng.dma_start(out=ac[f][:].bitcast(I32), in_=a_src[:, :, 2 * f * HALF : 2 * (f + 1) * HALF].bitcast(I32))

        def load_w(eng, f, g):
            eng.dma_start(
                out=wraw[f][g][:],
                in_=w[512 * g : 512 * (g + 1), f * HALF : (f + 1) * HALF].rearrange("(p j) n -> p j n", j=4),
            )

        def zero(plane):
            nc.vector.memset(plane[:].bitcast(I32), 0)

        zero(xs[0])
        zero(bsc[0])
        zero(asc[0])
        make_identity(nc, ident[:])

        nc.scalar.dma_start(out=h_rows[:], in_=h.rearrange("(p j) -> p j", p=P))
        load_plane(nc.sync, xs[0], x_scales, 0, 768, range(4))
        load_b_plane(nc.sync, 0, range(0, 1))
        load_x(nc.sync, 0)
        load_b(nc.sync, 0, 0)
        load_b_plane(nc.sync, 0, range(1, 4))
        load_b(nc.sync, 0, 1)
        load_a(nc.sync, 0)
        load_plane(nc.sync, asc[0], a_scales, 0, HALF, range(0, 1))
        load_w(nc.sync, 0, 0)
        load_plane(nc.sync, asc[0], a_scales, 0, HALF, range(1, 4))
        load_w(nc.sync, 0, 1)
        load_x(nc.sync, 1)
        zero(xs[1])
        zero(bsc[1])
        zero(asc[1])
        load_plane(nc.sync, xs[1], x_scales, 768, M, range(4))
        load_x(nc.sync, 2)
        load_w(nc.sync, 1, 0)
        load_w(nc.sync, 1, 1)
        load_plane(nc.sync, asc[1], a_scales, HALF, N, range(4))
        load_b_plane(nc.sync, 1, range(4))
        load_b(nc.sync, 1, 0)
        load_b(nc.sync, 1, 1)
        load_a(nc.sync, 1)

        def spread_h():
            bank = psum.tile([P, 4, P], F32, name="turned", tag="turned", bufs=2)
            words = h_rows[:].bitcast(F32)
            for j in range(4):
                nc.tensor.transpose(bank[:, j, :], words[:, j : j + 1].to_broadcast([P, P]), ident[:])
            nc.scalar.copy(
                out=h_all[:].bitcast(F32).rearrange("m (p j) -> m p j", j=4),
                in_=bank[:].rearrange("m j p -> m p j"),
            )

        def w_views(f, g, lo, hi):
            return (
                wgrp[f][g][:, 4 * lo : 4 * hi].rearrange("p (c i t) -> p c t i", i=4, t=4),
                wraw[f][g][:, :, lo:hi].rearrange("p t (c i) -> p c t i", i=4),
            )

        def group_w_scalar(f, g, lo, hi):
            dst, src = w_views(f, g, lo, hi)
            nc.scalar.activation(out=dst, in_=src, func=ACT.Copy)

        def group_w_gpsimd(f, g, lo, hi):
            dst = wgrp[f][g][:, 4 * lo : 4 * hi].rearrange("p (c t) -> p c t", t=4)
            src = wraw[f][g][:, :, lo:hi].rearrange("p t c -> p c t")
            nc.gpsimd.tensor_scalar(out=dst, in0=src, scalar1=1.0, scalar2=0.0, op0=ALU.mult, op1=ALU.add)

        def group_w_vector(f, g, lo, hi):
            dst, src = w_views(f, g, lo, hi)
            nc.vector.tensor_copy(out=dst, in_=src)

        def quantize_w(f, g):
            nc.vector.quantize_mx(out=wc[f][g][:].bitcast(FP8X4), scales=wsc[f][g][:], in_=wgrp[f][g][:])

        def x_operand(u, g):
            m0 = (u % ROW_TILES) * P
            i = [lo <= m0 < hi for lo, hi in X_CHUNKS].index(True)
            j = [lo <= m0 < hi for lo, hi in XS_CHUNKS].index(True)
            c0 = m0 - X_CHUNKS[i][0]
            s0 = m0 - XS_CHUNKS[j][0]
            return xc[i][:, g, c0 : c0 + P].bitcast(FP8X4), xs[j][:, g, s0 : s0 + P]

        def product(u, moving):
            bank = psum.tile([P, HALF], F32, name="acc", tag="acc", bufs=6)
            for g in range(PASSES):
                codes, scales = x_operand(u, g)
                rhs, rhs_scale = moving(u // ROW_TILES, g)
                nc.tensor.matmul_mx(
                    out=bank[:], lhsT=codes, lhsT_scale=scales, rhs=rhs, rhs_scale=rhs_scale,
                    start=(g == 0), stop=(g == PASSES - 1),
                )
            return bank

        def a_operand(f, g):
            return ac[f][:, g, :].bitcast(FP4X4), asc[f][:, g, :]

        def b_operand(f, g):
            return bc[f][g][:].bitcast(FP8X4), bsc[f][4 + 4 * g :, :]

        def w_operand(f, g):
            return wc[f][g][:].bitcast(FP8X4), wsc[f][g][:]

        shifted, metric, mean, y, rounded, grouped = {}, {}, {}, {}, {}, {}

        def do_q(u):
            f = u // ROW_TILES
            bank = product(u, b_operand)
            shifted[u] = work.tile([P, HALF], F32, name="shifted", bufs=3)
            nc.vector.tensor_tensor(out=shifted[u][:], in0=h_all[:, f * HALF : (f + 1) * HALF], in1=bank[:], op=ALU.subtract)

        def do_p(u):
            bank = product(u, a_operand)
            metric[u] = work.tile([P, HALF], F32, name="metric", bufs=8)
            nc.vector.tensor_tensor(out=metric[u][:], in0=bank[:], in1=shifted[u][:], op=ALU.add)

        def do_tanh(u):
            mean[u] = work.tile([P, HALF], F32, name="mean", bufs=8)
            nc.scalar.activation(out=mean[u][:], in_=metric[u][:], func=ACT.Tanh)

        def do_r(u, direct=False):
            f, mt = divmod(u, ROW_TILES)
            bank = product(u, w_operand)
            if direct:
                rounded[u] = work.tile([P, HALF], BF16, name="rounded", bufs=8, align_bytes=64)
                nc.vector.tensor_tensor(
                    out=rounded[u][:].rearrange("m (v p e) -> m v p e", v=2, e=2),
                    in0=bank[:].rearrange("m (p v e) -> m v p e", v=2, e=2),
                    in1=mean[u][:].rearrange("m (p v e) -> m v p e", v=2, e=2),
                    op=ALU.mult,
                )
            y[u] = work.tile([P, HALF], F32, name="y", bufs=8)
            nc.vector.tensor_tensor(out=y[u][:], in0=bank[:], in1=mean[u][:], op=ALU.mult)
            nc.sync.dma_start(out=out_0[mt * P : (mt + 1) * P, f * HALF : (f + 1) * HALF], in_=y[u][:])

        def do_r_aside(u, round_here):
            f, mt = divmod(u, ROW_TILES)
            bank = product(u, w_operand)
            readout = work.tile([P, HALF], F32, name="readout", bufs=2)
            nc.scalar.copy(out=readout[:], in_=bank[:])
            y[u] = work.tile([P, HALF], F32, name="y", bufs=8)
            for lo in range(0, HALF, HALF // 2):
                cols = slice(lo, lo + HALF // 2)
                nc.gpsimd.tensor_tensor(out=y[u][:, cols], in0=readout[:, cols], in1=mean[u][:, cols], op=ALU.mult)
            nc.sync.dma_start(out=out_0[mt * P : (mt + 1) * P, f * HALF : (f + 1) * HALF], in_=y[u][:])
            if round_here:
                rounded[u] = work.tile([P, HALF], BF16, name="rounded", bufs=8, align_bytes=64)
                nc.gpsimd.tensor_scalar(
                    out=rounded[u][:].rearrange("m (v p e) -> m v p e", v=2, e=2),
                    in0=y[u][:].rearrange("m (p v e) -> m v p e", v=2, e=2),
                    scalar1=1.0, scalar2=0.0, op0=ALU.mult, op1=ALU.add,
                )

        def do_round(u):
            rounded[u] = work.tile([P, HALF], BF16, name="rounded", bufs=8, align_bytes=64)
            nc.scalar.copy(
                out=rounded[u][:].rearrange("m (v p e) -> m v p e", v=2, e=2),
                in_=y[u][:].rearrange("m (p v e) -> m v p e", v=2, e=2),
            )

        turned = {}

        def do_turn(i):
            u0, count = GROUPS[i]
            if i == len(GROUPS) - 1:
                turned[i] = psum.tile([P, 4, P], F32, name="acc", tag="acc", bufs=6)
            else:
                turned[i] = psum.tile([P, 4, P], F32, name="turned", tag="turned", bufs=2)
            for j in range(count):
                words = rounded[u0 + j][:].bitcast(F32)
                for v in range(2):
                    nc.tensor.transpose(turned[i][:, 2 * j + v, :], words[:, v * P : (v + 1) * P], ident[:])

        quad_codes = {}

        def do_group(i):
            u0, count = GROUPS[i]
            if u0 % 4 == 0:
                grouped[u0 // 4] = work.tile([P, 4 * HALF], BF16, name="grouped", bufs=2, align_bytes=64)
            w0 = 2 * P * (u0 % 4)
            nc.scalar.copy(
                out=grouped[u0 // 4][:].bitcast(F32)[:, w0 : w0 + 2 * P * count].rearrange("p (j m v) -> p j m v", j=count, v=2),
                in_=turned[i][:, 0 : 2 * count, :].rearrange("p (j v) m -> p j m v", v=2),
            )

        def do_planes(u0, count):
            f, mt = divmod(u0, ROW_TILES)
            if u0 % 4 == 0:
                quad_codes[u0 // 4] = work.tile([P, HALF], U32, name="codes", bufs=3, align_bytes=64)
            c0 = (u0 % 4) * P
            nc.vector.quantize_mx(
                out=quad_codes[u0 // 4][:, c0 : c0 + count * P].bitcast(FP8X4),
                scales=ysc[f][:, mt * P : (mt + count) * P],
                in_=grouped[u0 // 4][:, 4 * c0 : 4 * (c0 + count * P)],
            )

        def store_codes(u0, count):
            f, mt = divmod(u0, ROW_TILES)
            c0 = (u0 % 4) * P
            nc.sync.dma_start(
                out=out_1[f].rearrange("p m t -> p (m t)")[:, 4 * mt * P : 4 * (mt + count) * P].bitcast(I32),
                in_=quad_codes[u0 // 4][:, c0 : c0 + count * P].bitcast(I32),
            )

        def store_scales(f, m0, m1, engines):
            for q in range(4):
                engines[q].dma_start(
                    out=out_2[f, 4 * q : 4 * q + 4, m0:m1].bitcast(I32),
                    in_=ysc[f][32 * q : 32 * q + 4, m0:m1].bitcast(I32),
                )

        spread_h()
        group_w_scalar(0, 0, 0, HALF // 2)
        group_w_scalar(0, 1, 0, HALF)
        do_q(0)
        do_q(1)
        do_p(0)
        group_w_vector(0, 0, HALF // 2, HALF)
        do_q(2)
        quantize_w(0, 0)
        do_p(1)
        quantize_w(0, 1)
        do_q(3)
        do_p(2)
        do_q(4)
        do_p(3)
        for u in range(4):
            do_tanh(u)
        for g in range(PASSES):
            for lo in range(0, HALF, P):
                group_w_gpsimd(1, g, lo, lo + P)
        do_r(0)
        do_p(4)
        do_r(1)
        do_round(0)
        do_round(1)
        do_tanh(4)
        aside = {8: True, 9: True, 12: True, 13: True, 16: True}
        late_round = {}
        turn_at = {8: (0, 1), 11: (2, 3), 15: (4, 5), 19: (6, 7), 21: (8,), 23: (9,)}
        group_at = {}
        for s, run in turn_at.items():
            for late, i in enumerate(run):
                group_at[s + late] = i
        planes_at = {10: (0, 4), 14: (4, 4), 18: (8, 4), 21: (12, 4)}
        w_at = {}
        wq_at = {8: 0, 9: 1}
        next_r = 2
        for s in range(5, UNITS):
            do_q(s)
            for i in turn_at.get(s, ()):
                do_turn(i)
            if s in group_at:
                do_group(group_at[s])
            done = late_round.get(s, [])
            if s in planes_at:
                do_planes(*planes_at[s])
                store_codes(*planes_at[s])
                if planes_at[s][0] + planes_at[s][1] == 12:
                    store_scales(0, 0, M, [nc.sync] * 4)
            for slot in range(2):
                if slot == 0 or s - next_r >= LAG:
                    if next_r in aside:
                        do_r_aside(next_r, aside[next_r])
                        if not aside[next_r]:
                            late_round[s + 1] = late_round.get(s + 1, []) + [next_r]
                    else:
                        done.append(next_r)
                        do_r(next_r)
                    next_r = next_r + 1
                if slot == 0:
                    do_p(s)
            for u in done:
                do_round(u)
            do_tanh(s)
            for fn, g, piece in w_at.get(s, ()):
                fn(1, g, piece * P, (piece + 1) * P)
            if s in wq_at:
                quantize_w(1, wq_at[s])
            if s == 22:
                do_planes(16, 2)
                store_codes(16, 2)
                store_scales(1, 0, 768, [nc.sync] * 4)
        do_r(22)
        do_planes(18, 2)
        store_codes(18, 2)
        do_round(22)
        do_r(23, direct=True)
        do_turn(10)
        do_turn(11)
        do_group(10)
        do_turn(12)
        do_group(11)
        do_group(12)
        do_planes(20, 2)
        do_planes(22, 1)
        do_planes(23, 1)
        store_codes(20, 4)
        store_scales(1, 768, M, [nc.sync, nc.scalar, nc.sync, nc.scalar])
